import numpy as np
import ml_dtypes

BF16 = ml_dtypes.bfloat16


def bf(x):
    return np.asarray(x, np.float32).astype(BF16)


def f32(x):
    return np.asarray(x, np.float32)


def f64(x):
    return np.asarray(x).astype(np.float64)


def striped(idx):
    return np.tile(idx.reshape(-1, 16).T, (8, 1))


S, K, M, N, E, Q = 512, 256, 128, 1024, 4, 256


def two_experts():
    first = np.random.permutation(S).reshape(E, S // E)
    return np.concatenate([np.random.permutation(np.concatenate([first[e], first[(e + 1) % E]])) for e in range(E)])


def setup_inputs():
    return {"table": bf(np.random.standard_normal((S, K))), "w": bf(np.random.standard_normal((E, K, M)) / np.sqrt(K)), "c": f32(0.2 + 0.8 * np.random.random_sample((1, N))), "offs": striped(two_experts())}


def reference(table, w, c, offs):
    idx = offs[:16].T.reshape(-1)
    x = f64(table)[idx].T
    y = np.concatenate([f64(w)[e].T @ x[:, e * Q : (e + 1) * Q] for e in range(E)], axis=1)
    return y * f64(c)

@@ -1,0 +1,67 @@
+import concourse.mybir as mybir
+from concourse.masks import make_identity
+
+BF16, F32, U16 = mybir.dt.bfloat16, mybir.dt.float32, mybir.dt.uint16
+
+P = 128
+S, K, M, N, E = 512, 256, 128, 1024, 4
+Q = N // E
+TOKEN_BLOCKS = S // P
+K_BLOCKS = K // P
+OFFSETS_PER_COLUMN = 16
+
+FLOPS = 2 * K * M * N
+
+
+def tile_gather_matmul_kernel(tc, table, w, c, offs, out):
+    nc = tc.nc
+    with (
+        tc.tile_pool(name="held", bufs=1) as held,
+        tc.psum_pool(name="flip", bufs=1) as flip,
+        tc.psum_pool(name="sums", bufs=1) as sums,
+    ):
+        offsets = held.tile([P, N // OFFSETS_PER_COLUMN], U16, name="offsets")
+        nc.sync.dma_start(offsets[:], offs)
+
+        token_rows = [held.tile([P, K], BF16, name=f"token_rows{t}") for t in range(TOKEN_BLOCKS)]
+        for t in range(TOKEN_BLOCKS):
+            queue = nc.sync if t % 2 == 0 else nc.scalar
+            queue.dma_start(token_rows[t][:], table[t * P : (t + 1) * P, :])
+
+        weights = held.tile([P, E * K_BLOCKS, M], BF16, name="weights")
+        nc.scalar.dma_start(weights[:], w.rearrange("e (b p) m -> p (e b) m", p=P))
+
+        factor = held.tile([P, N], F32, name="factor")
+        nc.gpsimd.dma_start(factor[:], c.broadcast_to([P, N]))
+
+        identity = held.tile([P, P], BF16, name="identity")
+        make_identity(nc, identity[:])
+
+        features = [held.tile([P, S], BF16, name=f"features{b}") for b in range(K_BLOCKS)]
+        for b in range(K_BLOCKS):
+            flipped = flip.tile([P, S], BF16, name=f"flipped{b}")
+            for t in range(TOKEN_BLOCKS):
+                nc.tensor.transpose(
+                    flipped[:, t * P : (t + 1) * P], token_rows[t][:, b * P : (b + 1) * P], identity[:]
+                )
+            if b % 2 == 0:
+                nc.vector.tensor_copy(features[b][:], flipped[:])
+            else:
+                nc.scalar.copy(features[b][:], flipped[:])
+
+        result = held.tile([P, N], F32, name="result")
+        for e in range(E):
+            piece = slice(e * Q, (e + 1) * Q)
+            piece_offsets = offsets[:, e * Q // OFFSETS_PER_COLUMN : (e + 1) * Q // OFFSETS_PER_COLUMN]
+            y = sums.tile([P, Q], F32, name=f"y{e}")
+            for b in range(K_BLOCKS):
+                nc.tensor.matmul(
+                    y[:],
+                    weights[:, e * K_BLOCKS + b, :],
+                    features[b][:].indirect(piece_offsets),
+                    start=(b == 0),
+                    stop=(b == K_BLOCKS - 1),
+                )
+            nc.vector.tensor_tensor(result[:, piece], y[:], factor[:, piece], mybir.AluOpType.mult)
+            queue = nc.sync if e % 2 == 0 else nc.scalar
+            queue.dma_start(out[:, piece], result[:, piece])

@@ -20,19 +20,19 @@ def tile_gather_matmul_kernel(tc, table, w, c, offs, out):
         tc.psum_pool(name="flip", bufs=1) as flip,
         tc.psum_pool(name="sums", bufs=1) as sums,
     ):
-        offsets = held.tile([P, N // OFFSETS_PER_COLUMN], U16, name="offsets")
-        nc.sync.dma_start(offsets[:], offs)
 
         token_rows = [held.tile([P, K], BF16, name=f"token_rows{t}") for t in range(TOKEN_BLOCKS)]
         for t in range(TOKEN_BLOCKS):
-            queue = nc.sync if t % 2 == 0 else nc.scalar
-            queue.dma_start(token_rows[t][:], table[t * P : (t + 1) * P, :])
+            nc.sync.dma_start(token_rows[t][:], table[t * P : (t + 1) * P, :])
+
+        offsets = held.tile([P, N // OFFSETS_PER_COLUMN], U16, name="offsets")
+        nc.sync.dma_start(offsets[:], offs)
 
         weights = held.tile([P, E * K_BLOCKS, M], BF16, name="weights")
-        nc.scalar.dma_start(weights[:], w.rearrange("e (b p) m -> p (e b) m", p=P))
+        nc.sync.dma_start(weights[:], w.rearrange("e (b p) m -> p (e b) m", p=P))
 
         factor = held.tile([P, N], F32, name="factor")
-        nc.gpsimd.dma_start(factor[:], c.broadcast_to([P, N]))
+        nc.sync.dma_start(factor[:], c.broadcast_to([P, N]))
 
         identity = held.tile([P, P], BF16, name="identity")
         make_identity(nc, identity[:])
@@ -49,19 +49,21 @@ def tile_gather_matmul_kernel(tc, table, w, c, offs, out):
             else:
                 nc.scalar.copy(features[b][:], flipped[:])
 
-        result = held.tile([P, N], F32, name="result")
-        for e in range(E):
-            piece = slice(e * Q, (e + 1) * Q)
-            piece_offsets = offsets[:, e * Q // OFFSETS_PER_COLUMN : (e + 1) * Q // OFFSETS_PER_COLUMN]
-            y = sums.tile([P, Q], F32, name=f"y{e}")
-            for b in range(K_BLOCKS):
+        y = [sums.tile([P, Q], F32, name=f"y{e}") for e in range(E)]
+        for b in range(K_BLOCKS):
+            for e in range(E):
+                piece_offsets = offsets[:, e * Q // OFFSETS_PER_COLUMN : (e + 1) * Q // OFFSETS_PER_COLUMN]
                 nc.tensor.matmul(
-                    y[:],
+                    y[e][:],
                     weights[:, e * K_BLOCKS + b, :],
                     features[b][:].indirect(piece_offsets),
                     start=(b == 0),
                     stop=(b == K_BLOCKS - 1),
                 )
-            nc.vector.tensor_tensor(result[:, piece], y[:], factor[:, piece], mybir.AluOpType.mult)
+
+        result = held.tile([P, N], F32, name="result")
+        for e in range(E):
+            piece = slice(e * Q, (e + 1) * Q)
+            nc.vector.tensor_tensor(result[:, piece], y[e][:], factor[:, piece], mybir.AluOpType.mult)
             queue = nc.sync if e % 2 == 0 else nc.scalar
             queue.dma_start(out[:, piece], result[:, piece])

@@ -9,6 +9,11 @@ Q = N // E
 TOKEN_BLOCKS = S // P
 K_BLOCKS = K // P
 OFFSETS_PER_COLUMN = 16
+B = 32
+C_ROWS = N // B
+assert C_ROWS == B
+WARMUP_COLUMNS = 512
+WARMUP_MATMULS = 3
 
 FLOPS = 2 * K * M * N
 
@@ -19,6 +24,7 @@ def tile_gather_matmul_kernel(tc, table, w, c, offs, out):
         tc.tile_pool(name="held", bufs=1) as held,
         tc.psum_pool(name="flip", bufs=1) as flip,
         tc.psum_pool(name="sums", bufs=1) as sums,
+        tc.psum_pool(name="warm", bufs=1) as warm,
     ):
 
         token_rows = [held.tile([P, K], BF16, name=f"token_rows{t}") for t in range(TOKEN_BLOCKS)]
@@ -31,11 +37,26 @@ def tile_gather_matmul_kernel(tc, table, w, c, offs, out):
         weights = held.tile([P, E * K_BLOCKS, M], BF16, name="weights")
         nc.sync.dma_start(weights[:], w.rearrange("e (b p) m -> p (e b) m", p=P))
 
-        factor = held.tile([P, N], F32, name="factor")
-        nc.sync.dma_start(factor[:], c.broadcast_to([P, N]))
+        c_rows = held.tile([P, B], F32, name="c_rows", align_bytes=64)
+        nc.scalar.dma_start(c_rows[:], c.rearrange("o (r q) -> o r q", q=B).to_broadcast([P // B, C_ROWS, B]))
 
         identity = held.tile([P, P], BF16, name="identity")
         make_identity(nc, identity[:])
+
+        zeros = held.tile([P, WARMUP_COLUMNS], BF16, name="zeros")
+        nc.vector.memset(zeros[:], 0.0)
+        unread = warm.tile([P, WARMUP_COLUMNS], F32, name="unread")
+        for i in range(WARMUP_MATMULS):
+            nc.tensor.matmul(unread[:], zeros[:, 0:P], zeros[:], start=True, stop=True)
+
+        c_cols = held.tile([P, C_ROWS], F32, name="c_cols", align_bytes=64)
+        nc.vector.transpose(c_cols[:], c_rows[:])
+        spread = held.tile([P, N], F32, name="spread", align_bytes=64)
+        nc.vector.tensor_copy(
+            spread[:].rearrange("p (r i) -> p r i", i=B), c_cols[:].unsqueeze(2).to_broadcast([P, C_ROWS, B])
+        )
+        factor = held.tile([P, N], F32, name="factor", align_bytes=64)
+        nc.vector.transpose(factor[:], spread[:])
 
         features = [held.tile([P, S], BF16, name=f"features{b}") for b in range(K_BLOCKS)]
         for b in range(K_BLOCKS):
@@ -44,10 +65,7 @@ def tile_gather_matmul_kernel(tc, table, w, c, offs, out):
                 nc.tensor.transpose(
                     flipped[:, t * P : (t + 1) * P], token_rows[t][:, b * P : (b + 1) * P], identity[:]
                 )
-            if b % 2 == 0:
-                nc.vector.tensor_copy(features[b][:], flipped[:])
-            else:
-                nc.scalar.copy(features[b][:], flipped[:])
+            nc.scalar.copy(features[b][:], flipped[:])
 
         y = [sums.tile([P, Q], F32, name=f"y{e}") for e in range(E)]
         for b in range(K_BLOCKS):

@@ -27,9 +27,8 @@ def tile_gather_matmul_kernel(tc, table, w, c, offs, out):
         tc.psum_pool(name="warm", bufs=1) as warm,
     ):
 
-        token_rows = [held.tile([P, K], BF16, name=f"token_rows{t}") for t in range(TOKEN_BLOCKS)]
-        for t in range(TOKEN_BLOCKS):
-            nc.sync.dma_start(token_rows[t][:], table[t * P : (t + 1) * P, :])
+        token_rows = held.tile([P, TOKEN_BLOCKS, K], BF16, name="token_rows")
+        nc.sync.dma_start(token_rows[:], table.rearrange("(t p) k -> p t k", p=P))
 
         offsets = held.tile([P, N // OFFSETS_PER_COLUMN], U16, name="offsets")
         nc.sync.dma_start(offsets[:], offs)
@@ -63,7 +62,7 @@ def tile_gather_matmul_kernel(tc, table, w, c, offs, out):
             flipped = flip.tile([P, S], BF16, name=f"flipped{b}")
             for t in range(TOKEN_BLOCKS):
                 nc.tensor.transpose(
-                    flipped[:, t * P : (t + 1) * P], token_rows[t][:, b * P : (b + 1) * P], identity[:]
+                    flipped[:, t * P : (t + 1) * P], token_rows[:, t, b * P : (b + 1) * P], identity[:]
                 )
             nc.scalar.copy(features[b][:], flipped[:])
 

@@ -82,5 +82,4 @@ def tile_gather_matmul_kernel(tc, table, w, c, offs, out):
         for e in range(E):
             piece = slice(e * Q, (e + 1) * Q)
             nc.vector.tensor_tensor(result[:, piece], y[e][:], factor[:, piece], mybir.AluOpType.mult)
-            queue = nc.sync if e % 2 == 0 else nc.scalar
-            queue.dma_start(out[:, piece], result[:, piece])
+            nc.sync.dma_start(out[:, piece], result[:, piece])

@@ -13,6 +13,7 @@ B = 32
 C_ROWS = N // B
 assert C_ROWS == B
 WARMUP_COLUMNS = 512
+WARMUP_REPEATS = WARMUP_COLUMNS // P
 WARMUP_MATMULS = 3
 
 FLOPS = 2 * K * M * N
@@ -39,14 +40,20 @@ def tile_gather_matmul_kernel(tc, table, w, c, offs, out):
         c_rows = held.tile([P, B], F32, name="c_rows", align_bytes=64)
         nc.scalar.dma_start(c_rows[:], c.rearrange("o (r q) -> o r q", q=B).to_broadcast([P // B, C_ROWS, B]))
 
+        zeros = held.tile([P, P], BF16, name="zeros")
+        nc.gpsimd.memset(zeros[:], 0.0)
         identity = held.tile([P, P], BF16, name="identity")
         make_identity(nc, identity[:])
 
-        zeros = held.tile([P, WARMUP_COLUMNS], BF16, name="zeros")
-        nc.vector.memset(zeros[:], 0.0)
         unread = warm.tile([P, WARMUP_COLUMNS], F32, name="unread")
         for i in range(WARMUP_MATMULS):
-            nc.tensor.matmul(unread[:], zeros[:, 0:P], zeros[:], start=True, stop=True)
+            nc.tensor.matmul(
+                unread[:].rearrange("p (r n) -> p r n", n=P),
+                zeros[:],
+                zeros[:].unsqueeze(1).to_broadcast([P, WARMUP_REPEATS, P]),
+                start=True,
+                stop=True,
+            )
 
         c_cols = held.tile([P, C_ROWS], F32, name="c_cols", align_bytes=64)
         nc.vector.transpose(c_cols[:], c_rows[:])

import concourse.mybir as mybir
from concourse.masks import make_identity

BF16, F32, U16 = mybir.dt.bfloat16, mybir.dt.float32, mybir.dt.uint16

P = 128
S, K, M, N, E = 512, 256, 128, 1024, 4
Q = N // E
TOKEN_BLOCKS = S // P
K_BLOCKS = K // P
OFFSETS_PER_COLUMN = 16
B = 32
C_ROWS = N // B
assert C_ROWS == B
WARMUP_COLUMNS = 512
WARMUP_REPEATS = WARMUP_COLUMNS // P
WARMUP_MATMULS = 3

FLOPS = 2 * K * M * N


def tile_gather_matmul_kernel(tc, table, w, c, offs, out):
    nc = tc.nc
    with (
        tc.tile_pool(name="held", bufs=1) as held,
        tc.psum_pool(name="flip", bufs=1) as flip,
        tc.psum_pool(name="sums", bufs=1) as sums,
        tc.psum_pool(name="warm", bufs=1) as warm,
    ):

        token_rows = held.tile([P, TOKEN_BLOCKS, K], BF16, name="token_rows")
        nc.sync.dma_start(token_rows[:], table.rearrange("(t p) k -> p t k", p=P))

        offsets = held.tile([P, N // OFFSETS_PER_COLUMN], U16, name="offsets")
        nc.sync.dma_start(offsets[:], offs)

        weights = held.tile([P, E * K_BLOCKS, M], BF16, name="weights")
        nc.sync.dma_start(weights[:], w.rearrange("e (b p) m -> p (e b) m", p=P))

        c_rows = held.tile([P, B], F32, name="c_rows", align_bytes=64)
        nc.scalar.dma_start(c_rows[:], c.rearrange("o (r q) -> o r q", q=B).to_broadcast([P // B, C_ROWS, B]))

        zeros = held.tile([P, P], BF16, name="zeros")
        nc.gpsimd.memset(zeros[:], 0.0)
        identity = held.tile([P, P], BF16, name="identity")
        make_identity(nc, identity[:])

        unread = warm.tile([P, WARMUP_COLUMNS], F32, name="unread")
        for i in range(WARMUP_MATMULS):
            nc.tensor.matmul(
                unread[:].rearrange("p (r n) -> p r n", n=P),
                zeros[:],
                zeros[:].unsqueeze(1).to_broadcast([P, WARMUP_REPEATS, P]),
                start=True,
                stop=True,
            )

        c_cols = held.tile([P, C_ROWS], F32, name="c_cols", align_bytes=64)
        nc.vector.transpose(c_cols[:], c_rows[:])
        spread = held.tile([P, N], F32, name="spread", align_bytes=64)
        nc.vector.tensor_copy(
            spread[:].rearrange("p (r i) -> p r i", i=B), c_cols[:].unsqueeze(2).to_broadcast([P, C_ROWS, B])
        )
        factor = held.tile([P, N], F32, name="factor", align_bytes=64)
        nc.vector.transpose(factor[:], spread[:])

        features = [held.tile([P, S], BF16, name=f"features{b}") for b in range(K_BLOCKS)]
        for b in range(K_BLOCKS):
            flipped = flip.tile([P, S], BF16, name=f"flipped{b}")
            for t in range(TOKEN_BLOCKS):
                nc.tensor.transpose(
                    flipped[:, t * P : (t + 1) * P], token_rows[:, t, b * P : (b + 1) * P], identity[:]
                )
            nc.scalar.copy(features[b][:], flipped[:])

        y = [sums.tile([P, Q], F32, name=f"y{e}") for e in range(E)]
        for b in range(K_BLOCKS):
            for e in range(E):
                piece_offsets = offsets[:, e * Q // OFFSETS_PER_COLUMN : (e + 1) * Q // OFFSETS_PER_COLUMN]
                nc.tensor.matmul(
                    y[e][:],
                    weights[:, e * K_BLOCKS + b, :],
                    features[b][:].indirect(piece_offsets),
                    start=(b == 0),
                    stop=(b == K_BLOCKS - 1),
                )

        result = held.tile([P, N], F32, name="result")
        for e in range(E):
            piece = slice(e * Q, (e + 1) * Q)
            nc.vector.tensor_tensor(result[:, piece], y[e][:], factor[:, piece], mybir.AluOpType.mult)
            nc.sync.dma_start(out[:, piece], result[:, piece])
